import numpy as np, ml_dtypes
CORES = [4,20,36,44,92,100,108,116,3,19,35,43,91,99,107,115]
N = 16
import mx_ref
NC, G = 128, 2
C = np.float32(0.029)
BF = ml_dtypes.bfloat16
def cut(t, i, w=512):
    return t[:, w * i:w * i + w]
def tile(rs):
    return np.stack(rs, axis=2).reshape(128, -1).astype(BF)
def layer(w, X):
    out = []
    for i in range(G):
        for t in range(len(X)):
            p = mx_ref.matmul(mx_ref.quantize(cut(w, len(X) * i + t)), X[t])
            z = p if t == 0 else z + p
        out.append(z)
    return out
def act(Z):
    return [np.maximum(s * z, 0) * C for z in Z for s in (1, -1)]
def turned(R):
    return [np.concatenate([R[b][:, 128 * t:128 * t + 128].T for b in range(4)], axis=1) for t in range(4)]
def setup_inputs(rng):
    def f(*shape):
        return mx_ref.flush((rng.standard_normal(shape, dtype=np.float32) * np.exp2(rng.integers(-2, 3, shape[:-1] + (1,)))).astype(BF))
    return {"x": f(N, 128, 4 * 512), "w1": f(N, 128, G * 512), "w2": f(N, 128, 512), "e": f(N, 128, 4 * NC)}
def setup_inputs_blocks(rng):
    d = setup_inputs(rng)
    for k in ("x", "w1", "w2", "e"): d[k] = mx_ref.spread(d[k], rng, 4)
    return d
def setup_inputs_wide(rng):
    d = setup_inputs(rng)
    for k in ("x", "w1", "w2", "e"): d[k] = mx_ref.flush((d[k].astype(np.float32) * np.exp2(rng.integers(-6, 7, (N, 1, 1))).astype(np.float32)).astype(BF))
    return d
def setup_inputs_zeros(rng):
    d = setup_inputs(rng); v = d["x"].reshape(N, 128, -1, 4).copy()
    v[np.broadcast_to((rng.random((N, 1, v.shape[2], 1)) < 0.33), v.shape)] = 0
    d["x"] = v.reshape(d["x"].shape)
    return d
def reference(x, w1, w2, e):
    R = [act(layer(w1[j], [mx_ref.quantize(x[j])])) for j in range(N)]
    H = [mx_ref.quantize(tile(R[j])) for j in range(N)]
    K = [tile(turned(R[j])) for j in range(N)]
    y = np.zeros((N, 128, 512), np.float32); z = np.zeros((N, 128, 4 * NC), np.float32)
    for r in range(N):
        y[r] = mx_ref.matmul(mx_ref.quantize(w2[r]), H[(r - 1) % N]); qe = mx_ref.quantize(e[r])
        for b in range(4):
            z[r][:, NC * b:NC * b + NC] = mx_ref.matmul(mx_ref.quantize(cut(K[(r + 1) % N], b)), qe)
    return {"y": y, "z": z}

@@ -1,0 +1,234 @@
+from concourse.bass import DstId, RemoteDMATransfer
+from concourse.mybir import dt, AluOpType, ActivationFunctionType
+
+C = 0.029
+HALF = 256
+POS = {0: 0, 2: 1, 1: 2, 3: 3}
+BF, F8, U8, F32 = "bfloat16", "float8_e4m3fn_x4", "uint8", "float32"
+
+SCRATCH = {
+    "bw1": ("sbuf", [128, 1024], BF), "bx": ("sbuf", [128, 2048], BF),
+    "bw2": ("sbuf", [128, 512], BF), "be": ("sbuf", [128, 512], BF),
+    "qw1": ("sbuf", [128, 256], F8), "sw1": ("sbuf", [128, 256], U8),
+    "qx": ("sbuf", [128, 512], F8), "sx": ("sbuf", [128, 512], U8),
+    "qw2": ("sbuf", [128, 128], F8), "sw2": ("sbuf", [128, 128], U8),
+    "qe": ("sbuf", [128, 128], F8), "se": ("sbuf", [128, 128], U8),
+    "th": ("sbuf", [128, 2048], BF), "tk": ("sbuf", [128, 2048], BF),
+    "qh": ("sbuf", [128, 512], F8), "sh": ("sbuf", [128, 512], U8),
+    "qk": ("sbuf", [128, 512], F8), "sk": ("sbuf", [128, 512], U8),
+    "lqh": ("sbuf", [128, 512], F8), "lsh": ("sbuf", [128, 512], U8),
+    "lqk": ("sbuf", [128, 512], F8), "lsk": ("sbuf", [128, 512], U8),
+    "oy": ("sbuf", [128, 512], F32), "oz": ("sbuf", [128, 512], F32),
+}
+for _b in range(8):
+    SCRATCH["p%d" % _b] = ("psum", [128, 512], F32)
+
+PIECES = [("q", 0, HALF, 0), ("q", HALF, 2 * HALF, 1), ("s", 0, 2 * HALF, 1)]
+
+SEMAPHORES = (["ld_w1", "ld_x0", "ld_x1", "ld_w2", "ld_e", "dq_w1", "dq_x0", "dq_x1", "dq_w2", "dq_e"]
+              + ["m%d" % b for b in range(8)]
+              + ["r_%s%d" % (t, c) for t in "hk" for c in range(2)]
+              + ["d_%s%d" % (t, c) for t in "hk" for c in range(2)]
+              + ["a_%s%d" % (t, i) for t in "hk" for i in range(len(PIECES))]
+              + ["n%s%d" % (t, i) for t in "yz" for i in range(4)]
+              + ["c%s%d" % (t, i) for t in "yz" for i in range(2)]
+              + ["st_%s%d" % (t, i) for t in "yz" for i in range(2)]
+              + ["sent"])
+
+
+def _bits(m):
+    return bin(m).count("1")
+
+
+def _routes(T, topo):
+    cores = list(T.cores)
+    n = len(cores)
+    used = set(cores)
+    out = {}
+    for r in range(n):
+        for tile, d in (("h", 1), ("k", -1)):
+            a, b = cores[r], cores[(r + d) % n]
+            if topo.may_write(a, b):
+                out[r, tile] = [a, b]
+                continue
+            for m in range(8 * n):
+                if (m not in used and topo.chip(m) == topo.chip(a) and topo.die(m) == topo.die(a) and topo.may_write(m, b)):
+                    used.add(m)
+                    out[r, tile] = [a, m, b]
+                    break
+    return out
+
+
+def _order(routes, r):
+    return ["k", "h"] if len(routes[r, "k"]) > len(routes[r, "h"]) else ["h", "k"]
+
+
+def _late(routes, r, tile):
+    return 2 * (len(routes[r, tile]) - 2) + 2 * _order(routes, r).index(tile)
+
+
+def _view(T, base, tile, kind, a, b):
+    v = T[base + kind + tile][:, a:b]
+    return v.bitcast(dt.uint8) if kind == "q" else v
+
+
+def _send(g, T, topo, src, dst, base, tile, i):
+    kind, a, b, _ = PIECES[i]
+    rid, pid, _s = topo.addr(dst)
+    mask = topo.mask(src, dst)
+    g.remote_dma(_view(T, "l", tile, kind, a, b), _view(T, base, tile, kind, a, b),
+                 T.sem["a_%s%d" % (tile, i)], T.sem.sent, pid, rid, mask)
+    return _bits(mask)
+
+
+def _forward(g, core, T, topo, routes):
+    for (r, tile), way in routes.items():
+        if len(way) == 3 and way[1] == core:
+            sent = 0
+            for i in range(len(PIECES)):
+                g.wait_ge(T.sem["a_%s%d" % (tile, i)], _bits(topo.mask(way[0], core)))
+                sent += _send(g, T, topo, core, way[2], "l", tile, i)
+            g.wait_ge(T.sem.sent, sent)
+
+
+def rank_program(g, core, T, topo):
+    routes = _routes(T, topo)
+    r = T.rank_of(core)
+    if r is None:
+        _forward(g, core, T, topo, routes)
+        return
+    n = len(T.cores)
+    S = T.sem
+    order = _order(routes, r)
+    relu, copy = ActivationFunctionType.Relu, ActivationFunctionType.Copy
+    mult, mx = AluOpType.mult, AluOpType.max
+
+    g.sync.dma_start(T.bw1[:], T.w1[:]).then_inc(S.ld_w1, 16)
+    g.scalar.dma_start(T.bx[:, 0:1024], T.x[:, 0:1024]).then_inc(S.ld_x0, 16)
+    g.sync.dma_start(T.bx[:, 1024:2048], T.x[:, 1024:2048]).then_inc(S.ld_x1, 16)
+    g.sync.wait_ge(S.ld_x1, 16)
+    g.sync.dma_start(T.bw2[:], T.w2[:]).then_inc(S.ld_w2, 16)
+    g.sync.dma_start(T.be[:], T.e[:]).then_inc(S.ld_e, 16)
+
+    g.vector.wait_ge(S.ld_w1, 16)
+    g.vector.quantize_mx(T.qw1[:, :], T.sw1[:, :], T.bw1[:, :]).then_inc(S.dq_w1, 1)
+    g.vector.wait_ge(S.ld_x0, 16)
+    g.vector.quantize_mx(T.qx[:, 0:256], T.sx[:, 0:256], T.bx[:, 0:1024]).then_inc(S.dq_x0, 1)
+    g.vector.wait_ge(S.ld_x1, 16)
+    g.vector.quantize_mx(T.qx[:, 256:512], T.sx[:, 256:512], T.bx[:, 1024:2048]).then_inc(S.dq_x1, 1)
+
+    def first(b):
+        if b < 4:
+            c, i = divmod(b, 2)
+            ws, xs = slice(128 * i, 128 * i + 128), slice(HALF * c, HALF * c + HALF)
+            call = g.tensor.matmul_mx(T["p%d" % b][:, 0:HALF], T.qw1[:, ws], T.sw1[:, ws], T.qx[:, xs], T.sx[:, xs], True, True)
+        else:
+            xs = slice(128 * (b - 4), 128 * (b - 4) + 128)
+            call = g.tensor.matmul_mx(T["p%d" % b][:, 0:HALF], T.qx[:, xs], T.sx[:, xs], T.qw1[:, :], T.sw1[:, :], True, True)
+        call.then_inc(S["m%d" % b], 1)
+
+    banks = {"h": [0, 1, 2, 3], "k": [4, 5, 6, 7]}
+    g.tensor.wait_ge(S.dq_w1, 1)
+    g.tensor.wait_ge(S.dq_x0, 1)
+    for b in banks[order[0]][:2]:
+        first(b)
+    g.tensor.wait_ge(S.dq_x1, 1)
+    for b in banks[order[0]][2:] + banks[order[1]]:
+        first(b)
+
+    seen = {"v": set(), "s": set()}
+
+    def cast(q, b, neg):
+        eng = g.vector if q == "v" else g.scalar
+        if b not in seen[q]:
+            seen[q].add(b)
+            eng.wait_ge(S["m%d" % b], 1)
+        if b < 4:
+            c, i = divmod(b, 2)
+            out, sem = T.th[:, 1024 * c + 2 * i + neg:1024 * (c + 1):4], S["r_h%d" % c]
+        else:
+            out, sem = T.tk[:, 1024 * neg + b - 4:1024 * (neg + 1):4], S["r_k%d" % neg]
+        src, f = T["p%d" % b][:, 0:HALF], -C if neg else C
+        if q == "v":
+            g.vector.tensor_scalar(out, src, f, 0.0, mult, mx).then_inc(sem, 1)
+        else:
+            g.scalar.activation(out, src, relu, scale=f).then_inc(sem, 1)
+
+    def pack(tile, c):
+        g.vector.wait_ge(S["r_%s%d" % (tile, c)], 4)
+        a, b = HALF * c, HALF * c + HALF
+        g.vector.quantize_mx(T["q" + tile][:, a:b], T["s" + tile][:, a:b], T["t" + tile][:, 4 * a:4 * b]).then_inc(S["d_%s%d" % (tile, c)], 1)
+
+    for tile in order:
+        if tile == "h":
+            for c in range(2):
+                for neg in range(2):
+                    cast("v", 2 * c, neg)
+                    cast("s", 2 * c + 1, neg)
+                pack("h", c)
+        elif order[0] == "k":
+            for neg in range(2):
+                cast("v", 4, neg)
+                cast("s", 5, neg)
+            for neg in range(2):
+                cast("v", 6, neg)
+                cast("s", 7, neg)
+                pack("k", neg)
+        else:
+            for neg in range(2):
+                cast("v", 4, neg)
+                for b in (5, 6, 7):
+                    cast("s", b, neg)
+                pack("k", neg)
+    g.vector.wait_ge(S.ld_w2, 16)
+    g.vector.quantize_mx(T.qw2[:, :], T.sw2[:, :], T.bw2[:, :]).then_inc(S.dq_w2, 1)
+    g.vector.wait_ge(S.ld_e, 16)
+    g.vector.quantize_mx(T.qe[:, :], T.se[:, :], T.be[:, :]).then_inc(S.dq_e, 1)
+
+    sent = 0
+    for tile in order:
+        nxt = routes[r, tile][1]
+        ready = -1
+        for i in range(len(PIECES)):
+            if PIECES[i][3] > ready:
+                ready = PIECES[i][3]
+                g.wait_ge(S["d_%s%d" % (tile, ready)], 1)
+            sent += _send(g, T, topo, core, nxt, "", tile, i)
+
+    u, v = (r - 1) % n, (r + 1) % n
+    turn = ["y", "z"] if _late(routes, u, "h") <= _late(routes, v, "k") else ["z", "y"]
+    for o in turn:
+        tile, way = ("h", routes[u, "h"]) if o == "y" else ("k", routes[v, "k"])
+        for c in range(2):
+            g.tensor.wait_ge(S["r_%s%d" % (tile, c)], 4)
+        g.tensor.wait_ge(S.dq_w2 if o == "y" else S.dq_e, 1)
+        for i in range(len(PIECES)):
+            g.tensor.wait_ge(S["a_%s%d" % (tile, i)], _bits(topo.mask(way[-2], core)))
+        if o == "y":
+            for c in range(2):
+                xs = slice(HALF * c, HALF * c + HALF)
+                g.tensor.matmul_mx(T["p%d" % c][:, 0:HALF], T.qw2[:, :], T.sw2[:, :], T.lqh[:, xs], T.lsh[:, xs], True, True).then_inc(S["ny%d" % c], 1)
+            g.vector.wait_ge(S.ny0, 1)
+            g.vector.tensor_copy(T.oy[:, 0:HALF], T.p0[:, 0:HALF]).then_inc(S.cy0, 1)
+            g.scalar.wait_ge(S.ny1, 1)
+            g.scalar.activation(T.oy[:, HALF:512], T.p1[:, 0:HALF], copy).then_inc(S.cy1, 1)
+            need, buf, dst = 1, T.oy, T.y
+        else:
+            for b in (0, 2, 1, 3):
+                ks = slice(128 * POS[b], 128 * POS[b] + 128)
+                g.tensor.matmul_mx(T["p%d" % (4 + b)][:, 0:128], T.lqk[:, ks], T.lsk[:, ks], T.qe[:, :], T.se[:, :], True, True).then_inc(S["nz%d" % b], 1)
+            for b in (0, 1):
+                g.vector.wait_ge(S["nz%d" % b], 1)
+                g.vector.tensor_copy(T.oz[:, 128 * b:128 * b + 128], T["p%d" % (4 + b)][:, 0:128]).then_inc(S.cz0, 1)
+            for b in (2, 3):
+                g.scalar.wait_ge(S["nz%d" % b], 1)
+                g.scalar.activation(T.oz[:, 128 * b:128 * b + 128], T["p%d" % (4 + b)][:, 0:128], copy).then_inc(S.cz1, 1)
+            need, buf, dst = 2, T.oz, T.z
+        g.sync.wait_ge(S["c%s0" % o], need)
+        g.sync.dma_start(dst[:, 0:256], buf[:, 0:256]).then_inc(S["st_%s0" % o], 16)
+        g.scalar.wait_ge(S["c%s1" % o], need)
+        g.scalar.dma_start(dst[:, 256:512], buf[:, 256:512]).then_inc(S["st_%s1" % o], 16)
+    for o in "yz":
+        for c in range(2):
+            g.sync.wait_ge(S["st_%s%d" % (o, c)], 16)
+    g.wait_ge(S.sent, sent)

@@ -1,9 +1,21 @@
-from concourse.bass import DstId, RemoteDMATransfer
 from concourse.mybir import dt, AluOpType, ActivationFunctionType
 
 C = 0.029
-HALF = 256
-POS = {0: 0, 2: 1, 1: 2, 3: 3}
+FIRST = {3: "k"}
+CUT_H = {"h": 192, "k": 256}
+CUT_K = {}
+LEAN = ((0, 0), (1, 1))
+KB = {256: ((0, 2), (1, 3)), 384: ((0, 2, 1), (3,))}
+WAYS = {
+    (2, "h"): (("near", 0), ("near", 1), ("near", 0)),
+    (3, "k"): (("near", 0), ("near", 1), ("near", 0)),
+    (4, "h"): (("near", 0), ("near", 1), ("near", 0)),
+    (5, "h"): (("near", 0), ("near", 1), ("near", 0)),
+    (5, "k"): (("far", 0), ("far", 1), ("far", 1)),
+    (6, "h"): (("far", 0), ("far", 0), ("far", 1)),
+    (6, "k"): (("near", 0), ("near", 1), ("near", 0)),
+    (7, "k"): (("near", 0), ("near", 1), ("near", 0)),
+}
 BF, F8, U8, F32 = "bfloat16", "float8_e4m3fn_x4", "uint8", "float32"
 
 SCRATCH = {
@@ -23,48 +35,63 @@ SCRATCH = {
 for _b in range(8):
     SCRATCH["p%d" % _b] = ("psum", [128, 512], F32)
 
-PIECES = [("q", 0, HALF, 0), ("q", HALF, 2 * HALF, 1), ("s", 0, 2 * HALF, 1)]
+SEMAPHORES = (["ld_w1", "ld_w2", "ld_e", "dq_w1", "dq_w2", "dq_e", "sent"]
+              + ["%s%d" % (s, c) for s in ("ld_x", "dq_x") for c in range(2)]
+              + ["mk%d" % b for b in range(4)] + ["mh%d" % b for b in range(4)]
+              + ["%s%s%d" % (s, t, c) for s in ("r_", "d_", "c", "st") for t in "hk" for c in range(2)]
+              + ["a_%s%d" % (t, i) for t in "hk" for i in range(3)]
+              + ["n%s%d" % (t, b) for t in "hk" for b in range(8)])
 
-SEMAPHORES = (["ld_w1", "ld_x0", "ld_x1", "ld_w2", "ld_e", "dq_w1", "dq_x0", "dq_x1", "dq_w2", "dq_e"]
-              + ["m%d" % b for b in range(8)]
-              + ["r_%s%d" % (t, c) for t in "hk" for c in range(2)]
-              + ["d_%s%d" % (t, c) for t in "hk" for c in range(2)]
-              + ["a_%s%d" % (t, i) for t in "hk" for i in range(len(PIECES))]
-              + ["n%s%d" % (t, i) for t in "yz" for i in range(4)]
-              + ["c%s%d" % (t, i) for t in "yz" for i in range(2)]
-              + ["st_%s%d" % (t, i) for t in "yz" for i in range(2)]
-              + ["sent"])
+
+def _order(r):
+    return ("k", "h") if FIRST.get(r) == "k" else ("h", "k")
+
+
+def _cut(r, tile):
+    return (0, CUT_H[_order(r)[0]], 512) if tile == "h" else (0, CUT_K.get(r, 256), 512)
+
+
+def _pieces(r, tile):
+    _, m, n = _cut(r, tile)
+    return (("q", 0, m, 1 if tile == "k" and m > 256 else 0), ("s", 0, n, 1), ("q", m, n, 1))
+
+
+def _owners(T, topo, chip, die):
+    per = [c for c in range(8 * len(T.cores)) if topo.chip(c) == chip]
+    mate = [c for c in range(8 * len(T.cores)) if topo.mates(topo.chip(c), chip)][0]
+    return sorted((c for c in per if c not in T.cores and topo.may_write(c, mate)), key=lambda c: topo.die(c) != die)
+
+
+def _way(T, topo, a, b, kind, j):
+    die = topo.die(a)
+    mid = b
+    if kind == "far":
+        over = [c for c in range(8 * len(T.cores)) if topo.mates(topo.chip(c), topo.chip(b))][0]
+        own = _owners(T, topo, topo.chip(over), die)
+        mid = own[j % len(own)]
+    way = [a]
+    if not topo.may_write(a, mid):
+        own = _owners(T, topo, topo.chip(a), die)
+        way.append(own[j % len(own)])
+    way.append(mid)
+    return way if mid == b else way + [b]
+
+
+def _routes(T, topo):
+    out = {}
+    n = len(T.cores)
+    for r in range(n):
+        for tile, d in (("h", 1), ("k", -1)):
+            out[r, tile] = [_way(T, topo, T.cores[r], T.cores[(r + d) % n], kind, j) for kind, j in WAYS.get((r, tile), (("near", 0),) * 3)]
+    return out
+
+
+def _due(routes, r, tile, c):
+    return 2 * max(len(w) - 2 for w in routes[r, tile]) + 2 * _order(r).index(tile) + 0.5 * c
 
 
 def _bits(m):
     return bin(m).count("1")
-
-
-def _routes(T, topo):
-    cores = list(T.cores)
-    n = len(cores)
-    used = set(cores)
-    out = {}
-    for r in range(n):
-        for tile, d in (("h", 1), ("k", -1)):
-            a, b = cores[r], cores[(r + d) % n]
-            if topo.may_write(a, b):
-                out[r, tile] = [a, b]
-                continue
-            for m in range(8 * n):
-                if (m not in used and topo.chip(m) == topo.chip(a) and topo.die(m) == topo.die(a) and topo.may_write(m, b)):
-                    used.add(m)
-                    out[r, tile] = [a, m, b]
-                    break
-    return out
-
-
-def _order(routes, r):
-    return ["k", "h"] if len(routes[r, "k"]) > len(routes[r, "h"]) else ["h", "k"]
-
-
-def _late(routes, r, tile):
-    return 2 * (len(routes[r, tile]) - 2) + 2 * _order(routes, r).index(tile)
 
 
 def _view(T, base, tile, kind, a, b):
@@ -72,23 +99,35 @@ def _view(T, base, tile, kind, a, b):
     return v.bitcast(dt.uint8) if kind == "q" else v
 
 
-def _send(g, T, topo, src, dst, base, tile, i):
-    kind, a, b, _ = PIECES[i]
-    rid, pid, _s = topo.addr(dst)
-    mask = topo.mask(src, dst)
-    g.remote_dma(_view(T, "l", tile, kind, a, b), _view(T, base, tile, kind, a, b),
-                 T.sem["a_%s%d" % (tile, i)], T.sem.sent, pid, rid, mask)
+def _mask(T, topo, routes, r, tile, i, j):
+    way = routes[r, tile][i]
+    m = topo.mask(way[j], way[j + 1])
+    if j == 0 and tile == _order(r)[1] and topo.chip(way[0]) == topo.chip(way[1]):
+        w = routes[r, _order(r)[0]][0]
+        if topo.chip(w[0]) != topo.chip(w[1]):
+            m &= ~topo.mask(w[0], w[1])
+    return m
+
+
+def _write(g, T, topo, routes, r, tile, i, j):
+    kind, a, b, _ = _pieces(r, tile)[i]
+    rid, pid, _s = topo.addr(routes[r, tile][i][j + 1])
+    mask = _mask(T, topo, routes, r, tile, i, j)
+    g.remote_dma(_view(T, "l", tile, kind, a, b), _view(T, "l" if j else "", tile, kind, a, b), T.sem["a_%s%d" % (tile, i)], T.sem.sent, pid, rid, mask)
     return _bits(mask)
 
 
 def _forward(g, core, T, topo, routes):
-    for (r, tile), way in routes.items():
-        if len(way) == 3 and way[1] == core:
-            sent = 0
-            for i in range(len(PIECES)):
-                g.wait_ge(T.sem["a_%s%d" % (tile, i)], _bits(topo.mask(way[0], core)))
-                sent += _send(g, T, topo, core, way[2], "l", tile, i)
-            g.wait_ge(T.sem.sent, sent)
+    sent = 0
+    for r in range(len(T.cores)):
+        for tile in _order(r):
+            for i, way in enumerate(routes[r, tile]):
+                if core in way[1:-1]:
+                    j = way.index(core)
+                    g.wait_ge(T.sem["a_%s%d" % (tile, i)], _bits(_mask(T, topo, routes, r, tile, i, j - 1)))
+                    sent += _write(g, T, topo, routes, r, tile, i, j)
+    if sent:
+        g.wait_ge(T.sem.sent, sent)
 
 
 def rank_program(g, core, T, topo):
@@ -99,56 +138,67 @@ def rank_program(g, core, T, topo):
         return
     n = len(T.cores)
     S = T.sem
-    order = _order(routes, r)
+    order = _order(r)
     relu, copy = ActivationFunctionType.Relu, ActivationFunctionType.Copy
     mult, mx = AluOpType.mult, AluOpType.max
+    xcut = _cut(r, "h")
 
     g.sync.dma_start(T.bw1[:], T.w1[:]).then_inc(S.ld_w1, 16)
-    g.scalar.dma_start(T.bx[:, 0:1024], T.x[:, 0:1024]).then_inc(S.ld_x0, 16)
-    g.sync.dma_start(T.bx[:, 1024:2048], T.x[:, 1024:2048]).then_inc(S.ld_x1, 16)
+    for c in range(2):
+        xs = slice(4 * xcut[c], 4 * xcut[c + 1])
+        (g.sync if c % 2 else g.scalar).dma_start(T.bx[:, xs], T.x[:, xs]).then_inc(S["ld_x%d" % c], 16)
     g.sync.wait_ge(S.ld_x1, 16)
     g.sync.dma_start(T.bw2[:], T.w2[:]).then_inc(S.ld_w2, 16)
     g.sync.dma_start(T.be[:], T.e[:]).then_inc(S.ld_e, 16)
 
     g.vector.wait_ge(S.ld_w1, 16)
     g.vector.quantize_mx(T.qw1[:, :], T.sw1[:, :], T.bw1[:, :]).then_inc(S.dq_w1, 1)
-    g.vector.wait_ge(S.ld_x0, 16)
-    g.vector.quantize_mx(T.qx[:, 0:256], T.sx[:, 0:256], T.bx[:, 0:1024]).then_inc(S.dq_x0, 1)
-    g.vector.wait_ge(S.ld_x1, 16)
-    g.vector.quantize_mx(T.qx[:, 256:512], T.sx[:, 256:512], T.bx[:, 1024:2048]).then_inc(S.dq_x1, 1)
+    for c in range(2):
+        g.vector.wait_ge(S["ld_x%d" % c], 16)
+        a, b = xcut[c], xcut[c + 1]
+        g.vector.quantize_mx(T.qx[:, a:b], T.sx[:, a:b], T.bx[:, 4 * a:4 * b]).then_inc(S["dq_x%d" % c], 1)
 
-    def first(b):
-        if b < 4:
-            c, i = divmod(b, 2)
-            ws, xs = slice(128 * i, 128 * i + 128), slice(HALF * c, HALF * c + HALF)
-            call = g.tensor.matmul_mx(T["p%d" % b][:, 0:HALF], T.qw1[:, ws], T.sw1[:, ws], T.qx[:, xs], T.sx[:, xs], True, True)
-        else:
-            xs = slice(128 * (b - 4), 128 * (b - 4) + 128)
-            call = g.tensor.matmul_mx(T["p%d" % b][:, 0:HALF], T.qx[:, xs], T.sx[:, xs], T.qw1[:, :], T.sw1[:, :], True, True)
-        call.then_inc(S["m%d" % b], 1)
+    have = [0]
 
-    banks = {"h": [0, 1, 2, 3], "k": [4, 5, 6, 7]}
+    def need_x(end):
+        while have[0] < 2 and xcut[have[0]] < end:
+            g.tensor.wait_ge(S["dq_x%d" % have[0]], 1)
+            have[0] += 1
+
+    def first_h():
+        for c in range(2):
+            need_x(xcut[c + 1])
+            for i in range(2):
+                st, mv = slice(128 * i, 128 * i + 128), slice(xcut[c], xcut[c + 1])
+                g.tensor.matmul_mx(T["p%d" % (2 * c + i)][:, 0:xcut[c + 1] - xcut[c]], T.qw1[:, st], T.sw1[:, st], T.qx[:, mv], T.sx[:, mv],
+                                   True, True).then_inc(S["mh%d" % (2 * c + i)], 1)
+
+    def first_k():
+        for t in range(4):
+            need_x(128 * t + 128)
+            st = slice(128 * t, 128 * t + 128)
+            g.tensor.matmul_mx(T["p%d" % (4 + t)][:, 0:256], T.qx[:, st], T.sx[:, st], T.qw1[:, :], T.sw1[:, :], True, True).then_inc(S["mk%d" % t], 1)
+
     g.tensor.wait_ge(S.dq_w1, 1)
-    g.tensor.wait_ge(S.dq_x0, 1)
-    for b in banks[order[0]][:2]:
-        first(b)
-    g.tensor.wait_ge(S.dq_x1, 1)
-    for b in banks[order[0]][2:] + banks[order[1]]:
-        first(b)
+    for tile in order:
+        first_h() if tile == "h" else first_k()
 
     seen = {"v": set(), "s": set()}
 
-    def cast(q, b, neg):
+    def cast(q, tile, j, neg):
         eng = g.vector if q == "v" else g.scalar
-        if b not in seen[q]:
-            seen[q].add(b)
-            eng.wait_ge(S["m%d" % b], 1)
-        if b < 4:
-            c, i = divmod(b, 2)
-            out, sem = T.th[:, 1024 * c + 2 * i + neg:1024 * (c + 1):4], S["r_h%d" % c]
+        m = "m%s%d" % (tile, j)
+        if m not in seen[q]:
+            seen[q].add(m)
+            eng.wait_ge(S[m], 1)
+        if tile == "h":
+            c, i = divmod(j, 2)
+            src = T["p%d" % j][:, 0:xcut[c + 1] - xcut[c]]
+            out, sem = T.th[:, 4 * xcut[c] + 2 * i + neg:4 * xcut[c + 1]:4], S["r_h%d" % c]
         else:
-            out, sem = T.tk[:, 1024 * neg + b - 4:1024 * (neg + 1):4], S["r_k%d" % neg]
-        src, f = T["p%d" % b][:, 0:HALF], -C if neg else C
+            src = T["p%d" % (4 + j)][:, 0:256]
+            out, sem = T.tk[:, 1024 * neg + j:1024 * (neg + 1):4], S["r_k%d" % neg]
+        f = -C if neg else C
         if q == "v":
             g.vector.tensor_scalar(out, src, f, 0.0, mult, mx).then_inc(sem, 1)
         else:
@@ -156,29 +206,35 @@ def rank_program(g, core, T, topo):
 
     def pack(tile, c):
         g.vector.wait_ge(S["r_%s%d" % (tile, c)], 4)
-        a, b = HALF * c, HALF * c + HALF
+        a, b = (xcut[c], xcut[c + 1]) if tile == "h" else (256 * c, 256 * c + 256)
         g.vector.quantize_mx(T["q" + tile][:, a:b], T["s" + tile][:, a:b], T["t" + tile][:, 4 * a:4 * b]).then_inc(S["d_%s%d" % (tile, c)], 1)
 
-    for tile in order:
+    for at, tile in enumerate(order):
         if tile == "h":
             for c in range(2):
-                for neg in range(2):
-                    cast("v", 2 * c, neg)
-                    cast("s", 2 * c + 1, neg)
+                cast("v", "h", 2 * c, 0)
+                cast("s", "h", 2 * c + 1, 0)
+                cast("s", "h", 2 * c + 1, 1)
+                if LEAN[at][c]:
+                    g.scalar.wait_ge(S["r_h%d" % c], 3)
+                cast("s" if LEAN[at][c] else "v", "h", 2 * c, 1)
                 pack("h", c)
-        elif order[0] == "k":
+        elif at == 0:
             for neg in range(2):
-                cast("v", 4, neg)
-                cast("s", 5, neg)
-            for neg in range(2):
-                cast("v", 6, neg)
-                cast("s", 7, neg)
-                pack("k", neg)
+                cast("v", "k", 0, neg)
+                cast("s", "k", 1, neg)
+            cast("v", "k", 2, 0)
+            cast("s", "k", 3, 0)
+            pack("k", 0)
+            cast("s", "k", 3, 1)
+            g.scalar.wait_ge(S.r_k0, 4)
+            cast("s", "k", 2, 1)
+            pack("k", 1)
         else:
             for neg in range(2):
-                cast("v", 4, neg)
-                for b in (5, 6, 7):
-                    cast("s", b, neg)
+                cast("v", "k", 0, neg)
+                for t in (1, 2, 3):
+                    cast("s", "k", t, neg)
                 pack("k", neg)
     g.vector.wait_ge(S.ld_w2, 16)
     g.vector.quantize_mx(T.qw2[:, :], T.sw2[:, :], T.bw2[:, :]).then_inc(S.dq_w2, 1)
@@ -187,48 +243,55 @@ def rank_program(g, core, T, topo):
 
     sent = 0
     for tile in order:
-        nxt = routes[r, tile][1]
         ready = -1
-        for i in range(len(PIECES)):
-            if PIECES[i][3] > ready:
-                ready = PIECES[i][3]
+        for i, piece in enumerate(_pieces(r, tile)):
+            while piece[3] > ready:
+                ready += 1
                 g.wait_ge(S["d_%s%d" % (tile, ready)], 1)
-            sent += _send(g, T, topo, core, nxt, "", tile, i)
+            sent += _write(g, T, topo, routes, r, tile, i, 0)
 
-    u, v = (r - 1) % n, (r + 1) % n
-    turn = ["y", "z"] if _late(routes, u, "h") <= _late(routes, v, "k") else ["z", "y"]
-    for o in turn:
-        tile, way = ("h", routes[u, "h"]) if o == "y" else ("k", routes[v, "k"])
-        for c in range(2):
-            g.tensor.wait_ge(S["r_%s%d" % (tile, c)], 4)
-        g.tensor.wait_ge(S.dq_w2 if o == "y" else S.dq_e, 1)
-        for i in range(len(PIECES)):
-            g.tensor.wait_ge(S["a_%s%d" % (tile, i)], _bits(topo.mask(way[-2], core)))
-        if o == "y":
-            for c in range(2):
-                xs = slice(HALF * c, HALF * c + HALF)
-                g.tensor.matmul_mx(T["p%d" % c][:, 0:HALF], T.qw2[:, :], T.sw2[:, :], T.lqh[:, xs], T.lsh[:, xs], True, True).then_inc(S["ny%d" % c], 1)
-            g.vector.wait_ge(S.ny0, 1)
-            g.vector.tensor_copy(T.oy[:, 0:HALF], T.p0[:, 0:HALF]).then_inc(S.cy0, 1)
-            g.scalar.wait_ge(S.ny1, 1)
-            g.scalar.activation(T.oy[:, HALF:512], T.p1[:, 0:HALF], copy).then_inc(S.cy1, 1)
-            need, buf, dst = 1, T.oy, T.y
+    src = {"h": (r - 1) % n, "k": (r + 1) % n}
+    come = set()
+    stores = {}
+    for _, tile, c in sorted((_due(routes, src[t], t, c), t, c) for t in "hk" for c in range(2)):
+        ways, cut = routes[src[tile], tile], _cut(src[tile], tile)
+        if c == 0:
+            for j in range(2):
+                g.tensor.wait_ge(S["r_%s%d" % (tile, j)], 4)
+            g.tensor.wait_ge(S.dq_w2 if tile == "h" else S.dq_e, 1)
+        a, b = cut[c], cut[c + 1]
+        for i, (kind, _a, end, _p) in enumerate(_pieces(src[tile], tile)):
+            if (tile, i) not in come and (kind == "s" or end <= b):
+                come.add((tile, i))
+                g.tensor.wait_ge(S["a_%s%d" % (tile, i)], _bits(_mask(T, topo, routes, src[tile], tile, i, len(ways[i]) - 2)))
+        done, stored = S["c%s%d" % (tile, c)], S["st%s%d" % (tile, c)]
+        if tile == "h":
+            mid = (a + b) // 2
+            jobs = [("v", a, mid, 2 * c, mid), ("s", mid, b, 2 * c + 1, b)] if mid - a >= 128 else [("v", a, b, 2 * c, b)]
+            outs = [(T.y, T.oy, a, b)]
         else:
-            for b in (0, 2, 1, 3):
-                ks = slice(128 * POS[b], 128 * POS[b] + 128)
-                g.tensor.matmul_mx(T["p%d" % (4 + b)][:, 0:128], T.lqk[:, ks], T.lsk[:, ks], T.qe[:, :], T.se[:, :], True, True).then_inc(S["nz%d" % b], 1)
-            for b in (0, 1):
-                g.vector.wait_ge(S["nz%d" % b], 1)
-                g.vector.tensor_copy(T.oz[:, 128 * b:128 * b + 128], T["p%d" % (4 + b)][:, 0:128]).then_inc(S.cz0, 1)
-            for b in (2, 3):
-                g.scalar.wait_ge(S["nz%d" % b], 1)
-                g.scalar.activation(T.oz[:, 128 * b:128 * b + 128], T["p%d" % (4 + b)][:, 0:128], copy).then_inc(S.cz1, 1)
-            need, buf, dst = 2, T.oz, T.z
-        g.sync.wait_ge(S["c%s0" % o], need)
-        g.sync.dma_start(dst[:, 0:256], buf[:, 0:256]).then_inc(S["st_%s0" % o], 16)
-        g.scalar.wait_ge(S["c%s1" % o], need)
-        g.scalar.dma_start(dst[:, 256:512], buf[:, 256:512]).then_inc(S["st_%s1" % o], 16)
-    for o in "yz":
-        for c in range(2):
-            g.sync.wait_ge(S["st_%s%d" % (o, c)], 16)
+            blks = KB[cut[1]][c]
+            jobs = [("vs"[j % 2], a + 128 * j, a + 128 * j + 128, 4 + blk, blk) for j, blk in enumerate(blks)]
+            outs = [(T.z, T.oz, 128 * blk, 128 * blk + 128) for blk in blks] if len(blks) < 3 else [(T.z, T.oz, 0, 384)]
+        for q, lo, hi, bank, blk in jobs:
+            cs = slice(lo, hi)
+            sem, p = S["n%s%d" % (tile, bank)], T["p%d" % bank][:, 0:hi - lo]
+            if tile == "h":
+                out = T.oy[:, cs]
+                g.tensor.matmul_mx(p, T.qw2[:, :], T.sw2[:, :], T.lqh[:, cs], T.lsh[:, cs], True, True).then_inc(sem, 1)
+            else:
+                out = T.oz[:, 128 * blk:128 * blk + 128]
+                g.tensor.matmul_mx(p, T.lqk[:, cs], T.lsk[:, cs], T.qe[:, :], T.se[:, :], True, True).then_inc(sem, 1)
+            if q == "v":
+                g.vector.wait_ge(sem, 1)
+                g.vector.tensor_copy(out, p).then_inc(done, 1)
+            else:
+                g.scalar.wait_ge(sem, 1)
+                g.scalar.activation(out, p, copy).then_inc(done, 1)
+        g.sync.wait_ge(done, len(jobs))
+        for to, frm, lo, hi in outs:
+            g.sync.dma_start(to[:, lo:hi], frm[:, lo:hi]).then_inc(stored, 16)
+        stores[tile, c] = 16 * len(outs)
+    for (tile, c), v in stores.items():
+        g.sync.wait_ge(S["st%s%d" % (tile, c)], v)
     g.wait_ge(S.sent, sent)

from concourse.mybir import dt, AluOpType, ActivationFunctionType

C = 0.029
FIRST = {3: "k"}
CUT_H = {"h": 192, "k": 256}
CUT_K = {}
LEAN = ((0, 0), (1, 1))
KB = {256: ((0, 2), (1, 3)), 384: ((0, 2, 1), (3,))}
WAYS = {
    (2, "h"): (("near", 0), ("near", 1), ("near", 0)),
    (3, "k"): (("near", 0), ("near", 1), ("near", 0)),
    (4, "h"): (("near", 0), ("near", 1), ("near", 0)),
    (5, "h"): (("near", 0), ("near", 1), ("near", 0)),
    (5, "k"): (("far", 0), ("far", 1), ("far", 1)),
    (6, "h"): (("far", 0), ("far", 0), ("far", 1)),
    (6, "k"): (("near", 0), ("near", 1), ("near", 0)),
    (7, "k"): (("near", 0), ("near", 1), ("near", 0)),
}
BF, F8, U8, F32 = "bfloat16", "float8_e4m3fn_x4", "uint8", "float32"

SCRATCH = {
    "bw1": ("sbuf", [128, 1024], BF), "bx": ("sbuf", [128, 2048], BF),
    "bw2": ("sbuf", [128, 512], BF), "be": ("sbuf", [128, 512], BF),
    "qw1": ("sbuf", [128, 256], F8), "sw1": ("sbuf", [128, 256], U8),
    "qx": ("sbuf", [128, 512], F8), "sx": ("sbuf", [128, 512], U8),
    "qw2": ("sbuf", [128, 128], F8), "sw2": ("sbuf", [128, 128], U8),
    "qe": ("sbuf", [128, 128], F8), "se": ("sbuf", [128, 128], U8),
    "th": ("sbuf", [128, 2048], BF), "tk": ("sbuf", [128, 2048], BF),
    "qh": ("sbuf", [128, 512], F8), "sh": ("sbuf", [128, 512], U8),
    "qk": ("sbuf", [128, 512], F8), "sk": ("sbuf", [128, 512], U8),
    "lqh": ("sbuf", [128, 512], F8), "lsh": ("sbuf", [128, 512], U8),
    "lqk": ("sbuf", [128, 512], F8), "lsk": ("sbuf", [128, 512], U8),
    "oy": ("sbuf", [128, 512], F32), "oz": ("sbuf", [128, 512], F32),
}
for _b in range(8):
    SCRATCH["p%d" % _b] = ("psum", [128, 512], F32)

SEMAPHORES = (["ld_w1", "ld_w2", "ld_e", "dq_w1", "dq_w2", "dq_e", "sent"]
              + ["%s%d" % (s, c) for s in ("ld_x", "dq_x") for c in range(2)]
              + ["mk%d" % b for b in range(4)] + ["mh%d" % b for b in range(4)]
              + ["%s%s%d" % (s, t, c) for s in ("r_", "d_", "c", "st") for t in "hk" for c in range(2)]
              + ["a_%s%d" % (t, i) for t in "hk" for i in range(3)]
              + ["n%s%d" % (t, b) for t in "hk" for b in range(8)])


def _order(r):
    return ("k", "h") if FIRST.get(r) == "k" else ("h", "k")


def _cut(r, tile):
    return (0, CUT_H[_order(r)[0]], 512) if tile == "h" else (0, CUT_K.get(r, 256), 512)


def _pieces(r, tile):
    _, m, n = _cut(r, tile)
    return (("q", 0, m, 1 if tile == "k" and m > 256 else 0), ("s", 0, n, 1), ("q", m, n, 1))


def _owners(T, topo, chip, die):
    per = [c for c in range(8 * len(T.cores)) if topo.chip(c) == chip]
    mate = [c for c in range(8 * len(T.cores)) if topo.mates(topo.chip(c), chip)][0]
    return sorted((c for c in per if c not in T.cores and topo.may_write(c, mate)), key=lambda c: topo.die(c) != die)


def _way(T, topo, a, b, kind, j):
    die = topo.die(a)
    mid = b
    if kind == "far":
        over = [c for c in range(8 * len(T.cores)) if topo.mates(topo.chip(c), topo.chip(b))][0]
        own = _owners(T, topo, topo.chip(over), die)
        mid = own[j % len(own)]
    way = [a]
    if not topo.may_write(a, mid):
        own = _owners(T, topo, topo.chip(a), die)
        way.append(own[j % len(own)])
    way.append(mid)
    return way if mid == b else way + [b]


def _routes(T, topo):
    out = {}
    n = len(T.cores)
    for r in range(n):
        for tile, d in (("h", 1), ("k", -1)):
            out[r, tile] = [_way(T, topo, T.cores[r], T.cores[(r + d) % n], kind, j) for kind, j in WAYS.get((r, tile), (("near", 0),) * 3)]
    return out


def _due(routes, r, tile, c):
    return 2 * max(len(w) - 2 for w in routes[r, tile]) + 2 * _order(r).index(tile) + 0.5 * c


def _bits(m):
    return bin(m).count("1")


def _view(T, base, tile, kind, a, b):
    v = T[base + kind + tile][:, a:b]
    return v.bitcast(dt.uint8) if kind == "q" else v


def _mask(T, topo, routes, r, tile, i, j):
    way = routes[r, tile][i]
    m = topo.mask(way[j], way[j + 1])
    if j == 0 and tile == _order(r)[1] and topo.chip(way[0]) == topo.chip(way[1]):
        w = routes[r, _order(r)[0]][0]
        if topo.chip(w[0]) != topo.chip(w[1]):
            m &= ~topo.mask(w[0], w[1])
    return m


def _write(g, T, topo, routes, r, tile, i, j):
    kind, a, b, _ = _pieces(r, tile)[i]
    rid, pid, _s = topo.addr(routes[r, tile][i][j + 1])
    mask = _mask(T, topo, routes, r, tile, i, j)
    g.remote_dma(_view(T, "l", tile, kind, a, b), _view(T, "l" if j else "", tile, kind, a, b), T.sem["a_%s%d" % (tile, i)], T.sem.sent, pid, rid, mask)
    return _bits(mask)


def _forward(g, core, T, topo, routes):
    sent = 0
    for r in range(len(T.cores)):
        for tile in _order(r):
            for i, way in enumerate(routes[r, tile]):
                if core in way[1:-1]:
                    j = way.index(core)
                    g.wait_ge(T.sem["a_%s%d" % (tile, i)], _bits(_mask(T, topo, routes, r, tile, i, j - 1)))
                    sent += _write(g, T, topo, routes, r, tile, i, j)
    if sent:
        g.wait_ge(T.sem.sent, sent)


def rank_program(g, core, T, topo):
    routes = _routes(T, topo)
    r = T.rank_of(core)
    if r is None:
        _forward(g, core, T, topo, routes)
        return
    n = len(T.cores)
    S = T.sem
    order = _order(r)
    relu, copy = ActivationFunctionType.Relu, ActivationFunctionType.Copy
    mult, mx = AluOpType.mult, AluOpType.max
    xcut = _cut(r, "h")

    g.sync.dma_start(T.bw1[:], T.w1[:]).then_inc(S.ld_w1, 16)
    for c in range(2):
        xs = slice(4 * xcut[c], 4 * xcut[c + 1])
        (g.sync if c % 2 else g.scalar).dma_start(T.bx[:, xs], T.x[:, xs]).then_inc(S["ld_x%d" % c], 16)
    g.sync.wait_ge(S.ld_x1, 16)
    g.sync.dma_start(T.bw2[:], T.w2[:]).then_inc(S.ld_w2, 16)
    g.sync.dma_start(T.be[:], T.e[:]).then_inc(S.ld_e, 16)

    g.vector.wait_ge(S.ld_w1, 16)
    g.vector.quantize_mx(T.qw1[:, :], T.sw1[:, :], T.bw1[:, :]).then_inc(S.dq_w1, 1)
    for c in range(2):
        g.vector.wait_ge(S["ld_x%d" % c], 16)
        a, b = xcut[c], xcut[c + 1]
        g.vector.quantize_mx(T.qx[:, a:b], T.sx[:, a:b], T.bx[:, 4 * a:4 * b]).then_inc(S["dq_x%d" % c], 1)

    have = [0]

    def need_x(end):
        while have[0] < 2 and xcut[have[0]] < end:
            g.tensor.wait_ge(S["dq_x%d" % have[0]], 1)
            have[0] += 1

    def first_h():
        for c in range(2):
            need_x(xcut[c + 1])
            for i in range(2):
                st, mv = slice(128 * i, 128 * i + 128), slice(xcut[c], xcut[c + 1])
                g.tensor.matmul_mx(T["p%d" % (2 * c + i)][:, 0:xcut[c + 1] - xcut[c]], T.qw1[:, st], T.sw1[:, st], T.qx[:, mv], T.sx[:, mv],
                                   True, True).then_inc(S["mh%d" % (2 * c + i)], 1)

    def first_k():
        for t in range(4):
            need_x(128 * t + 128)
            st = slice(128 * t, 128 * t + 128)
            g.tensor.matmul_mx(T["p%d" % (4 + t)][:, 0:256], T.qx[:, st], T.sx[:, st], T.qw1[:, :], T.sw1[:, :], True, True).then_inc(S["mk%d" % t], 1)

    g.tensor.wait_ge(S.dq_w1, 1)
    for tile in order:
        first_h() if tile == "h" else first_k()

    seen = {"v": set(), "s": set()}

    def cast(q, tile, j, neg):
        eng = g.vector if q == "v" else g.scalar
        m = "m%s%d" % (tile, j)
        if m not in seen[q]:
            seen[q].add(m)
            eng.wait_ge(S[m], 1)
        if tile == "h":
            c, i = divmod(j, 2)
            src = T["p%d" % j][:, 0:xcut[c + 1] - xcut[c]]
            out, sem = T.th[:, 4 * xcut[c] + 2 * i + neg:4 * xcut[c + 1]:4], S["r_h%d" % c]
        else:
            src = T["p%d" % (4 + j)][:, 0:256]
            out, sem = T.tk[:, 1024 * neg + j:1024 * (neg + 1):4], S["r_k%d" % neg]
        f = -C if neg else C
        if q == "v":
            g.vector.tensor_scalar(out, src, f, 0.0, mult, mx).then_inc(sem, 1)
        else:
            g.scalar.activation(out, src, relu, scale=f).then_inc(sem, 1)

    def pack(tile, c):
        g.vector.wait_ge(S["r_%s%d" % (tile, c)], 4)
        a, b = (xcut[c], xcut[c + 1]) if tile == "h" else (256 * c, 256 * c + 256)
        g.vector.quantize_mx(T["q" + tile][:, a:b], T["s" + tile][:, a:b], T["t" + tile][:, 4 * a:4 * b]).then_inc(S["d_%s%d" % (tile, c)], 1)

    for at, tile in enumerate(order):
        if tile == "h":
            for c in range(2):
                cast("v", "h", 2 * c, 0)
                cast("s", "h", 2 * c + 1, 0)
                cast("s", "h", 2 * c + 1, 1)
                if LEAN[at][c]:
                    g.scalar.wait_ge(S["r_h%d" % c], 3)
                cast("s" if LEAN[at][c] else "v", "h", 2 * c, 1)
                pack("h", c)
        elif at == 0:
            for neg in range(2):
                cast("v", "k", 0, neg)
                cast("s", "k", 1, neg)
            cast("v", "k", 2, 0)
            cast("s", "k", 3, 0)
            pack("k", 0)
            cast("s", "k", 3, 1)
            g.scalar.wait_ge(S.r_k0, 4)
            cast("s", "k", 2, 1)
            pack("k", 1)
        else:
            for neg in range(2):
                cast("v", "k", 0, neg)
                for t in (1, 2, 3):
                    cast("s", "k", t, neg)
                pack("k", neg)
    g.vector.wait_ge(S.ld_w2, 16)
    g.vector.quantize_mx(T.qw2[:, :], T.sw2[:, :], T.bw2[:, :]).then_inc(S.dq_w2, 1)
    g.vector.wait_ge(S.ld_e, 16)
    g.vector.quantize_mx(T.qe[:, :], T.se[:, :], T.be[:, :]).then_inc(S.dq_e, 1)

    sent = 0
    for tile in order:
        ready = -1
        for i, piece in enumerate(_pieces(r, tile)):
            while piece[3] > ready:
                ready += 1
                g.wait_ge(S["d_%s%d" % (tile, ready)], 1)
            sent += _write(g, T, topo, routes, r, tile, i, 0)

    src = {"h": (r - 1) % n, "k": (r + 1) % n}
    come = set()
    stores = {}
    for _, tile, c in sorted((_due(routes, src[t], t, c), t, c) for t in "hk" for c in range(2)):
        ways, cut = routes[src[tile], tile], _cut(src[tile], tile)
        if c == 0:
            for j in range(2):
                g.tensor.wait_ge(S["r_%s%d" % (tile, j)], 4)
            g.tensor.wait_ge(S.dq_w2 if tile == "h" else S.dq_e, 1)
        a, b = cut[c], cut[c + 1]
        for i, (kind, _a, end, _p) in enumerate(_pieces(src[tile], tile)):
            if (tile, i) not in come and (kind == "s" or end <= b):
                come.add((tile, i))
                g.tensor.wait_ge(S["a_%s%d" % (tile, i)], _bits(_mask(T, topo, routes, src[tile], tile, i, len(ways[i]) - 2)))
        done, stored = S["c%s%d" % (tile, c)], S["st%s%d" % (tile, c)]
        if tile == "h":
            mid = (a + b) // 2
            jobs = [("v", a, mid, 2 * c, mid), ("s", mid, b, 2 * c + 1, b)] if mid - a >= 128 else [("v", a, b, 2 * c, b)]
            outs = [(T.y, T.oy, a, b)]
        else:
            blks = KB[cut[1]][c]
            jobs = [("vs"[j % 2], a + 128 * j, a + 128 * j + 128, 4 + blk, blk) for j, blk in enumerate(blks)]
            outs = [(T.z, T.oz, 128 * blk, 128 * blk + 128) for blk in blks] if len(blks) < 3 else [(T.z, T.oz, 0, 384)]
        for q, lo, hi, bank, blk in jobs:
            cs = slice(lo, hi)
            sem, p = S["n%s%d" % (tile, bank)], T["p%d" % bank][:, 0:hi - lo]
            if tile == "h":
                out = T.oy[:, cs]
                g.tensor.matmul_mx(p, T.qw2[:, :], T.sw2[:, :], T.lqh[:, cs], T.lsh[:, cs], True, True).then_inc(sem, 1)
            else:
                out = T.oz[:, 128 * blk:128 * blk + 128]
                g.tensor.matmul_mx(p, T.lqk[:, cs], T.lsk[:, cs], T.qe[:, :], T.se[:, :], True, True).then_inc(sem, 1)
            if q == "v":
                g.vector.wait_ge(sem, 1)
                g.vector.tensor_copy(out, p).then_inc(done, 1)
            else:
                g.scalar.wait_ge(sem, 1)
                g.scalar.activation(out, p, copy).then_inc(done, 1)
        g.sync.wait_ge(done, len(jobs))
        for to, frm, lo, hi in outs:
            g.sync.dma_start(to[:, lo:hi], frm[:, lo:hi]).then_inc(stored, 16)
        stores[tile, c] = 16 * len(outs)
    for (tile, c), v in stores.items():
        g.sync.wait_ge(S["st%s%d" % (tile, c)], v)
    g.wait_ge(S.sent, sent)
